import numpy as np
import ml_dtypes


def mxq(x, axis, fmt="e4m3"):
    dtype, down = {"e4m3": (ml_dtypes.float8_e4m3fn, 7), "e5m2": (ml_dtypes.float8_e5m2, 14)}[fmt]
    v = np.moveaxis(np.asarray(x, np.float32).astype(ml_dtypes.bfloat16).astype(np.float64), axis, -1)
    blocks = v.reshape(v.shape[:-1] + (-1, 32))
    amax = np.abs(blocks).max(-1, keepdims=True)
    byte = np.maximum(np.where(amax > 0, np.frexp(amax)[1] - 1 + 127, 0) - down, 1)
    scale = np.exp2(byte - 127.0)
    codes = (blocks / scale).astype(np.float32).astype(dtype).astype(np.float64)
    return np.moveaxis((codes * scale).reshape(v.shape), -1, axis)


WIDE = False


def mx_kscale(k):
    if not WIDE:
        return np.ones(k)
    levels = np.array([10, -10, 5, -5, 0])
    if k % 512:
        return np.exp2(np.random.permutation(np.resize(levels, k // 32))).repeat(32)
    a = np.empty((k // 512, 16))
    for p in range(k // 512):
        a[p, :8] = np.random.permutation(np.resize(levels, 8))
        for g in range(8):
            far = levels[np.abs(levels - a[p, g]) >= 10]
            a[p, g + 8] = far[np.random.randint(len(far))]
    return np.exp2(a.ravel()).repeat(32)


BF16 = ml_dtypes.bfloat16


def bf(x):
    return np.asarray(x, np.float32).astype(BF16)


def f64(x):
    return np.asarray(x).astype(np.float64)


E2M1 = np.array([0.0, 0.5, 1.0, 1.5, 2.0, 3.0, 4.0, 6.0, -0.0, -0.5, -1.0, -1.5, -2.0, -3.0, -4.0, -6.0])


def pack_weight(w, fmt):
    k, n = w.shape
    w = f64(bf(w)).reshape(k // 32, 32, n)
    amax = np.abs(w).max(1)
    if fmt == "e4m3":
        byte = np.frexp(amax)[1] - 1 + 127 - 7
    else:
        mant, ex = np.frexp(amax / 6.0)
        byte = np.where(mant > 0.5, ex, ex - 1) + 127
    byte = np.clip(np.where(amax > 0, byte, 1), 1, 254)
    scaled = (w * np.exp2(127.0 - byte)[:, None, :]).reshape(k, n).astype(np.float32)
    by_word = np.ascontiguousarray(scaled.reshape(k // 512, 128, 4, n).transpose(0, 1, 3, 2))
    if fmt == "e4m3":
        words = by_word.astype(ml_dtypes.float8_e4m3fn).view(np.uint8)
    else:
        c = by_word.astype(ml_dtypes.float4_e2m1fn).view(np.uint8) & 0xF
        words = c[..., 0::2] | (c[..., 1::2] << 4)
    return np.ascontiguousarray(words), np.ascontiguousarray(byte.astype(np.uint8).reshape(k // 512, 16, n))


def unpack_weight(words, scales, fmt):
    g, p, n, _ = words.shape
    if fmt == "e4m3":
        vals = np.ascontiguousarray(words).view(ml_dtypes.float8_e4m3fn).astype(np.float64)
    else:
        nib = np.empty((g, p, n, 4), np.uint8)
        nib[..., 0::2] = words & 0xF
        nib[..., 1::2] = words >> 4
        vals = E2M1[nib]
    vals = vals * np.repeat(np.exp2(scales.astype(np.float64) - 127.0), 8, axis=1)[..., None]
    return vals.transpose(0, 1, 3, 2).reshape(g * 512, n)
def pack4(w):
    words, scales = pack_weight(w, "e2m1")
    return words.reshape(words.shape[0], 128, -1), scales


def unpack4(words, scales):
    return unpack_weight(words.reshape(words.shape[0], 128, -1, 2), scales, "e2m1")


E4M3FN = np.array([(-1.0 if i & 128 else 1.0) * ((1.0 + (i & 7) / 8.0) * 2.0 ** (((i >> 3) & 15) - 7) if i & 120 else (i & 7) * 2.0 ** -9) for i in range(256)])


def e4m3fn_bytes(y):
    return np.clip(np.asarray(y, np.float64), -448.0, 448.0).astype(np.float32).astype(ml_dtypes.float8_e4m3fn).view(np.uint8)


def e4m3fn_values(b):
    return E4M3FN[b]

def planes(Y):
    n, m = Y.shape
    b = f64(bf(Y)).reshape(n // 32, 32, m)
    amax = np.abs(b).max(1)
    byte = np.clip(np.where(amax > 0, np.frexp(amax)[1] - 1 + 127 - 7, 1), 1, 254)
    codes = (b * np.exp2(127.0 - byte)[:, None, :]).reshape(n, m).astype(np.float32).astype(ml_dtypes.float8_e4m3fn).view(np.uint8)
    words = codes.reshape(n // 512, 128, 4, m).transpose(0, 1, 3, 2)
    return np.ascontiguousarray(words), np.ascontiguousarray(byte.astype(np.uint8).reshape(n // 512, 16, m))


T, K, N, B = 1280, 1536, 1024, 128

def setup_inputs():
    s = mx_kscale(K)
    X = np.random.randn(T, K) * np.exp(0.3 * np.random.randn(T, 1)) * s[None, :]
    X_scale = (np.abs(X).reshape(T, K // B, B).max(axis=2) / 448.0).astype(np.float32)
    X_bytes = e4m3fn_bytes(X / np.repeat(f64(X_scale), B, axis=1))
    spread = np.exp(0.8 * np.random.randn(1, N))
    Wh = 0.6 * spread * np.random.randn(K, N) / np.sqrt(K) / s[:, None]
    Wg = np.random.randn(K, N) / np.sqrt(K) / s[:, None]
    Wh_words, Wh_scales = pack4(Wh)
    Wg_words, Wg_scales = pack4(Wg)
    return {
        "X_bytes": X_bytes, "X_scale": X_scale,
        "Wh_words": Wh_words, "Wh_scales": Wh_scales,
        "Wg_words": Wg_words, "Wg_scales": Wg_scales,
        "b_gate": bf(0.5 * (np.random.randn(1, N) - 1.0)),
        "carry": bf(0.5 * spread * np.random.randn(T, N)),
    }

def reference(X_bytes, X_scale, Wh_words, Wh_scales, Wg_words, Wg_scales, b_gate, carry):
    X = e4m3fn_values(X_bytes) * np.repeat(f64(X_scale), B, axis=1)
    xq = mxq(X, 1, "e4m3")
    Wh = unpack4(Wh_words, Wh_scales)
    Wg = unpack4(Wg_words, Wg_scales)
    cand = np.tanh(xq @ Wh)
    gate = 1.0 / (1.0 + np.exp(-((xq @ Wg) + f64(b_gate))))
    c = f64(carry)
    y = c + gate * (cand - c)
    words, scales = planes(y.T)
    return y, words, scales

@@ -1,0 +1,368 @@
+from contextlib import ExitStack
+
+import concourse.mybir as mybir
+from concourse.masks import make_identity
+
+T, K, N, B = 1280, 1536, 1024, 128
+FLOPS = 2 * 2 * T * K * N
+
+F32 = mybir.dt.float32
+BF16 = mybir.dt.bfloat16
+I32 = mybir.dt.int32
+U32 = mybir.dt.uint32
+U8 = mybir.dt.uint8
+FP8 = mybir.dt.float8_e4m3fn
+FP8X4 = mybir.dt.float8_e4m3fn_x4
+FP4X4 = mybir.dt.float4_e2m1fn_x4
+ALU = mybir.AluOpType
+ACT = mybir.ActivationFunctionType
+
+P = 128
+TILES = T // P
+PASSES = K // 512
+HALF = 512
+PAIRS = TILES * PASSES // 2
+HEAD_PAIRS = 7
+FIRST_STEP_PAIRS = 3
+FIRST_VECTOR_BLOCKS = 4
+LAST_WIDEN_STEP = 6
+OPENING_VECTOR_BLOCKS = 5
+HEAD_VECTOR_BLOCKS = 7
+LOOP_VECTOR_BLOCKS = 2
+STORE_BATCHES = ((0, 4), (4, 8), (8, 10))
+
+
+def tile_highway_gate_encode_b2_kernel(
+    tc, X_bytes, X_scale, Wh_words, Wh_scales, Wg_words, Wg_scales, b_gate, carry, out_0, out_1, out_2
+):
+    nc = tc.nc
+    with ExitStack() as ctx:
+        keep = ctx.enter_context(tc.tile_pool(name="keep", bufs=1))
+        work = ctx.enter_context(tc.tile_pool(name="work", bufs=2))
+        psum = ctx.enter_context(tc.psum_pool(name="psum", bufs=4))
+        ctx.enter_context(tc.manual_schedule())
+
+        ident = keep.tile([P, P], F32, name="ident")
+        make_identity(nc, ident[:])
+
+        x_scale = keep.tile([P, TILES, K // B], F32, name="x_scale")
+        nc.scalar.dma_start(out=x_scale[:], in_=X_scale.rearrange("(i p) j -> p i j", p=P))
+        ident_bf = keep.tile([P, P], BF16, name="ident_bf")
+        bias_rows = keep.tile([P, P], BF16, name="bias_rows")
+        nc.vector.memset(bias_rows[:], 0.0)
+        nc.scalar.dma_start(out=bias_rows[: N // P, :], in_=b_gate.rearrange("o (c j) -> (o c) j", j=P))
+        warm = keep.tile([P, 1], F32, name="warm")
+        nc.vector.memset(warm[:], 0.0)
+        w_scales = []
+        for name in ("wg_scales", "wh_scales"):
+            plane = keep.tile([P, PASSES, N], U8, name=name, align_bytes=64)
+            nc.vector.memset(plane[:].bitcast(U32), 0)
+            w_scales.insert(0, plane)
+        nc.scalar.activation(out=warm[:], in_=warm[:], func=ACT.Sigmoid)
+        nc.vector.tensor_copy(out=ident_bf[:], in_=ident[:])
+
+        x_raw = {}
+        carry_sb = {}
+        w_words = {}
+
+        def load_x(first, last):
+            raw = keep.tile([P, last - first, K], U8, name="x_raw%d" % first)
+            nc.sync.dma_start(out=raw[:], in_=X_bytes[first * P : last * P, :].rearrange("(i p) k -> p i k", p=P))
+            for i in range(first, last):
+                x_raw[i] = raw[:, i - first, :]
+
+        def load_carry(first, last):
+            tile = keep.tile([P, last - first, N], BF16, name="carry%d" % first)
+            nc.sync.dma_start(out=tile[:], in_=carry[first * P : last * P, :].rearrange("(i p) n -> p i n", p=P))
+            for i in range(first, last):
+                carry_sb[i] = tile[:, i - first, :]
+
+        def load_words(w, half):
+            tile = keep.tile([P, PASSES, 2 * HALF], U8, name="words%d_%d" % (w, half), align_bytes=64)
+            src = (Wh_words, Wg_words)[w][:, :, half * 2 * HALF : (half + 1) * 2 * HALF]
+            nc.sync.dma_start(out=tile[:].bitcast(I32), in_=src.rearrange("g p b -> p g b").bitcast(I32))
+            w_words[w, half] = tile
+
+        def load_scales(w):
+            for q in range(4):
+                src = (Wh_scales, Wg_scales)[w][:, 4 * q : 4 * q + 4, :]
+                nc.sync.dma_start(
+                    out=w_scales[w][32 * q : 32 * q + 4, :, :].bitcast(I32),
+                    in_=src.rearrange("g r n -> r g n").bitcast(I32),
+                )
+
+        load_x(0, 1)
+        load_x(1, 3)
+        load_x(3, 5)
+        load_scales(1)
+        load_scales(0)
+        load_words(1, 0)
+        load_words(1, 1)
+        load_x(5, 7)
+        load_words(0, 0)
+        load_words(0, 1)
+        load_carry(0, 1)
+        load_carry(1, 2)
+        load_x(7, TILES)
+        load_carry(2, 6)
+        load_carry(6, TILES)
+
+        bias = keep.tile([P, N], BF16, name="bias")
+
+        def bias_to_columns():
+            bank = psum.tile([P, P], BF16, name="acc")
+            nc.tensor.transpose(bank[:], bias_rows[:], ident_bf[:])
+            columns = keep.tile([P, N // P], BF16, name="bias_columns")
+            nc.vector.tensor_copy(out=columns[:], in_=bank[:, : N // P])
+            return columns
+
+        def spread_bias(columns):
+            bank = psum.tile([P, N], BF16, name="acc")
+            for c in range(N // P):
+                nc.tensor.transpose(bank[:, c * P : (c + 1) * P], columns[:, c : c + 1].to_broadcast([P, P]), ident_bf[:])
+            return bank
+
+        x_wide = {}
+        x_bank = {}
+        x_grouped = {}
+        x_codes = {}
+        x_planes = {}
+
+        def widen(pair, vector_blocks):
+            wide = work.tile([P, 2 * 512], BF16, name="x_wide", bufs=4)
+            for b in range(8):
+                i, j = divmod(8 * pair + b, K // B)
+                src = x_raw[i][:, j * B : (j + 1) * B].bitcast(FP8)
+                dst = wide[:, b * B : (b + 1) * B]
+                if b >= 8 - vector_blocks:
+                    nc.vector.tensor_scalar(
+                        out=dst, in0=src, scalar1=x_scale[:, i, j : j + 1], scalar2=None, op0=ALU.mult
+                    )
+                else:
+                    nc.scalar.activation(out=dst, in_=src, func=ACT.Copy, scale=x_scale[:, i, j : j + 1])
+            x_wide[pair] = wide
+
+        def turn_x(pair):
+            words = x_wide[pair][:].bitcast(F32)
+            bank = psum.tile([P, 4, P], F32, name="turn")
+            for s in range(4):
+                g, u = divmod(s, 2)
+                nc.tensor.transpose(bank[:, s, :], words[:, 256 * g + u : 256 * (g + 1) : 2], ident[:])
+            x_bank[pair] = bank
+
+        def empty_x(pair):
+            grouped = work.tile([P, 2 * 512], BF16, name="x_grouped", bufs=4, align_bytes=64)
+            nc.scalar.copy(
+                out=grouped[:].bitcast(F32).rearrange("p (g r u) -> p g r u", g=2, u=2),
+                in_=x_bank[pair][:].rearrange("p (g u) r -> p g r u", u=2),
+            )
+            x_grouped[pair] = grouped
+
+        def quantize_x(pair):
+            codes = keep.tile([P, 2 * P], U32, name="x_codes%d" % pair, align_bytes=64)
+            plane = keep.tile([P, 2 * P], U8, name="x_plane%d" % pair, align_bytes=64)
+            nc.vector.quantize_mx(out=codes[:].bitcast(FP8X4), scales=plane[:], in_=x_grouped[pair][:])
+            x_codes[pair] = codes
+            x_planes[pair] = plane
+
+        acc = {}
+
+        def multiply(i, w, half):
+            bank = psum.tile([P, HALF], F32, name="acc")
+            for g in range(PASSES):
+                pair, side = divmod(PASSES * i + g, 2)
+                cols = slice(side * P, (side + 1) * P)
+                nc.tensor.matmul_mx(
+                    out=bank[:],
+                    lhsT=x_codes[pair][:, cols].bitcast(FP8X4),
+                    lhsT_scale=x_planes[pair][:, cols],
+                    rhs=w_words[w, half][:, g, :].bitcast(FP4X4),
+                    rhs_scale=w_scales[w][:, g, half * HALF : (half + 1) * HALF],
+                    start=(g == 0),
+                    stop=(g == PASSES - 1),
+                )
+            acc[i, w, half] = bank
+
+        tiles = {}
+
+        def f32_tile(name, i, bufs=2):
+            if (name, i) not in tiles:
+                tiles[name, i] = work.tile([P, N], F32, name=name, bufs=bufs)
+            return tiles[name, i]
+
+        def cols_of(halves):
+            return slice(halves[0] * HALF, (halves[-1] + 1) * HALF)
+
+        def tanh(i, half):
+            nc.scalar.activation(out=f32_tile("cand", i)[:, cols_of([half])], in_=acc[i, 0, half][:], func=ACT.Tanh)
+
+        def add_bias(i, half):
+            c = cols_of([half])
+            nc.vector.tensor_tensor(out=f32_tile("pre", i)[:, c], in0=acc[i, 1, half][:], in1=bias[:, c], op=ALU.add)
+
+        def sigmoid(i, halves):
+            c = cols_of(halves)
+            nc.scalar.activation(out=f32_tile("gate", i)[:, c], in_=f32_tile("pre", i)[:, c], func=ACT.Sigmoid)
+
+        def subtract(i, halves):
+            c = cols_of(halves)
+            nc.vector.tensor_tensor(
+                out=f32_tile("diff", i)[:, c], in0=f32_tile("cand", i)[:, c], in1=carry_sb[i][:, c], op=ALU.subtract
+            )
+
+        def gate_mult(i, halves):
+            c = cols_of(halves)
+            nc.vector.tensor_tensor(
+                out=f32_tile("step", i)[:, c], in0=f32_tile("gate", i)[:, c], in1=f32_tile("diff", i)[:, c], op=ALU.mult
+            )
+
+        def add_carry(i, halves):
+            c = cols_of(halves)
+            y = f32_tile("y", i, 3)
+            nc.vector.tensor_tensor(out=y[:, c], in0=f32_tile("step", i)[:, c], in1=carry_sb[i][:, c], op=ALU.add)
+            nc.sync.dma_start(out=out_0[i * P : (i + 1) * P, c], in_=y[:, c])
+
+        y_round = {}
+        y_bank = {}
+        y_grouped = {}
+
+        def round_y(i, halves):
+            if i not in y_round:
+                y_round[i] = work.tile([P, N], BF16, name="y_round")
+            c = cols_of(halves)
+            nc.scalar.copy(
+                out=y_round[i][:, c].rearrange("m (g u p e) -> m g u p e", u=2, p=P, e=2),
+                in_=f32_tile("y", i, 3)[:, c].rearrange("m (g p u e) -> m g u p e", u=2, p=P, e=2),
+            )
+
+        def turn_y(i, halves):
+            words = y_round[i][:].bitcast(F32)
+            bank = psum.tile([P, 2 * len(halves), P], F32, name="turn")
+            for s in range(2 * len(halves)):
+                first = (2 * halves[0] + s) * P
+                nc.tensor.transpose(bank[:, s, :], words[:, first : first + P], ident[:])
+            y_bank[i, halves[0]] = bank
+
+        def empty_y(i, halves):
+            if i not in y_grouped:
+                y_grouped[i] = work.tile([P, N], BF16, name="y_grouped", bufs=3, align_bytes=64)
+            nc.scalar.copy(
+                out=y_grouped[i][:, cols_of(halves)].bitcast(F32).rearrange("p (g r u) -> p g r u", r=P, u=2),
+                in_=y_bank[i, halves[0]][:].rearrange("p (g u) r -> p g r u", u=2),
+            )
+
+        y_codes = {}
+        y_planes = {}
+        for first, last in STORE_BATCHES:
+            width = (last - first) * P
+            y_codes[first] = keep.tile([P, 2, width], U32, name="y_codes%d" % first, align_bytes=64)
+            y_planes[first] = keep.tile([P, 2, width], U8, name="y_plane%d" % first, align_bytes=64)
+
+        def quantize_y(i, halves):
+            first, last = [b for b in STORE_BATCHES if b[0] <= i < b[1]][0]
+            cols = slice((i - first) * P, (i - first + 1) * P)
+            for g in halves:
+                nc.vector.quantize_mx(
+                    out=y_codes[first][:, g, cols].bitcast(FP8X4),
+                    scales=y_planes[first][:, g, cols],
+                    in_=y_grouped[i][:, cols_of([g])],
+                )
+            if i == last - 1:
+                tokens = slice(first * P, last * P)
+                groups = slice(halves[0], halves[-1] + 1)
+                nc.sync.dma_start(
+                    out=out_1[groups, :, tokens, :].rearrange("g p m t -> p g (m t)").bitcast(I32),
+                    in_=y_codes[first][:, groups, :].bitcast(I32),
+                )
+            if i == last - 1 and halves[-1] == 1:
+                for q in range(4):
+                    queue = nc.scalar if (last == TILES and q % 2 == 0) else nc.sync
+                    queue.dma_start(
+                        out=out_2[:, 4 * q : 4 * q + 4, tokens].rearrange("g r m -> r g m").bitcast(I32),
+                        in_=y_planes[first][32 * q : 32 * q + 4, :, :].bitcast(I32),
+                    )
+
+        both = [0, 1]
+
+        order = ((1, 0), (1, 1), (0, 0), (0, 1))
+        for s in range(HEAD_PAIRS):
+            widen(s, OPENING_VECTOR_BLOCKS if s < 2 else HEAD_VECTOR_BLOCKS)
+            if s == 2:
+                columns = bias_to_columns()
+            if s == 3:
+                spread = spread_bias(columns)
+            turn_x(s)
+            if s >= 1:
+                empty_x(s - 1)
+            if s >= 3:
+                quantize_x(s - 3)
+        nc.scalar.copy(out=bias[:], in_=spread[:])
+        for w, half in order:
+            multiply(0, w, half)
+        empty_x(HEAD_PAIRS - 1)
+
+        last = TILES - 1
+        waiting = list(range(HEAD_PAIRS, HEAD_PAIRS + FIRST_STEP_PAIRS))
+        quantize_x(HEAD_PAIRS - 3)
+        widen(waiting[0], 8)
+        quantize_x(HEAD_PAIRS - 2)
+        add_bias(0, 0)
+        quantize_x(HEAD_PAIRS - 1)
+        add_bias(0, 1)
+        widen(waiting[1], FIRST_VECTOR_BLOCKS)
+        widen(waiting[2], FIRST_VECTOR_BLOCKS)
+        tanh(0, 0)
+        tanh(0, 1)
+        for w, half in order:
+            multiply(1, w, half)
+        sigmoid(0, both)
+        subtract(0, both)
+        for s in range(1, TILES):
+            turned = waiting
+            waiting = [p for p in range(HEAD_PAIRS + FIRST_STEP_PAIRS, PAIRS) if p - PAIRS + LAST_WIDEN_STEP + 1 == s]
+            for pair in turned:
+                turn_x(pair)
+            if s >= 2:
+                turn_y(s - 2, both)
+            add_bias(s, 0)
+            gate_mult(s - 1, both)
+            add_bias(s, 1)
+            tanh(s, 0)
+            tanh(s, 1)
+            if s < last:
+                for w, half in order:
+                    multiply(s + 1, w, half)
+            for pair in turned:
+                empty_x(pair)
+            if s < last:
+                sigmoid(s, both)
+            else:
+                sigmoid(s, [0])
+                sigmoid(s, [1])
+            add_carry(s - 1, both)
+            if s >= 3:
+                quantize_y(s - 3, both)
+            if s >= 2:
+                empty_y(s - 2, both)
+            subtract(s, both)
+            round_y(s - 1, both)
+            for pair in waiting:
+                widen(pair, LOOP_VECTOR_BLOCKS)
+            for pair in turned:
+                quantize_x(pair)
+        quantize_y(last - 2, both)
+        turn_y(last - 1, both)
+        gate_mult(last, [0])
+        gate_mult(last, [1])
+        add_carry(last, [0])
+        empty_y(last - 1, both)
+        round_y(last, [0])
+        turn_y(last, [0])
+        add_carry(last, [1])
+        quantize_y(last - 1, both)
+        round_y(last, [1])
+        turn_y(last, [1])
+        empty_y(last, [0])
+        empty_y(last, [1])
+        quantize_y(last, [0])
+        quantize_y(last, [1])

@@ -29,7 +29,10 @@ LAST_WIDEN_STEP = 6
 OPENING_VECTOR_BLOCKS = 5
 HEAD_VECTOR_BLOCKS = 7
 LOOP_VECTOR_BLOCKS = 2
-STORE_BATCHES = ((0, 4), (4, 8), (8, 10))
+BIAS_ROWS = N // (2 * P)
+WIDEN_STEPS = (0, 1, 3, 5, 6)
+CODE_BATCHES = ((0, 4), (4, 7), (7, 9), (9, 10))
+SCALE_BATCHES = ((0, 7), (7, 10))
 
 
 def tile_highway_gate_encode_b2_kernel(
@@ -45,12 +48,22 @@ def tile_highway_gate_encode_b2_kernel(
         ident = keep.tile([P, P], F32, name="ident")
         make_identity(nc, ident[:])
 
-        x_scale = keep.tile([P, TILES, K // B], F32, name="x_scale")
-        nc.scalar.dma_start(out=x_scale[:], in_=X_scale.rearrange("(i p) j -> p i j", p=P))
-        ident_bf = keep.tile([P, P], BF16, name="ident_bf")
-        bias_rows = keep.tile([P, P], BF16, name="bias_rows")
+        x_scale = {}
+
+        def load_x_scale(first, last, queue):
+            tile = keep.tile([P, last - first, 16], F32, name="x_scale%d" % first)
+            queue.dma_start(
+                out=tile[:, :, : K // B], in_=X_scale[first * P : last * P, :].rearrange("(i p) j -> p i j", p=P)
+            )
+            for i in range(first, last):
+                x_scale[i] = tile[:, i - first, :]
+
+        load_x_scale(0, 3, nc.scalar)
+        bias_rows = keep.tile([P, P], F32, name="bias_rows")
         nc.vector.memset(bias_rows[:], 0.0)
-        nc.scalar.dma_start(out=bias_rows[: N // P, :], in_=b_gate.rearrange("o (c j) -> (o c) j", j=P))
+        nc.scalar.dma_start(
+            out=bias_rows[:BIAS_ROWS, :].bitcast(BF16), in_=b_gate.rearrange("o (c j) -> (o c) j", c=BIAS_ROWS)
+        )
         warm = keep.tile([P, 1], F32, name="warm")
         nc.vector.memset(warm[:], 0.0)
         w_scales = []
@@ -59,7 +72,6 @@ def tile_highway_gate_encode_b2_kernel(
             nc.vector.memset(plane[:].bitcast(U32), 0)
             w_scales.insert(0, plane)
         nc.scalar.activation(out=warm[:], in_=warm[:], func=ACT.Sigmoid)
-        nc.vector.tensor_copy(out=ident_bf[:], in_=ident[:])
 
         x_raw = {}
         carry_sb = {}
@@ -93,33 +105,36 @@ def tile_highway_gate_encode_b2_kernel(
 
         load_x(0, 1)
         load_x(1, 3)
-        load_x(3, 5)
         load_scales(1)
-        load_scales(0)
         load_words(1, 0)
-        load_words(1, 1)
-        load_x(5, 7)
+        load_x_scale(3, TILES, nc.sync)
+        load_x(3, 5)
+        load_scales(0)
         load_words(0, 0)
+        load_x(5, 7)
+        load_words(1, 1)
         load_words(0, 1)
         load_carry(0, 1)
-        load_carry(1, 2)
         load_x(7, TILES)
+        load_carry(1, 2)
         load_carry(2, 6)
         load_carry(6, TILES)
 
         bias = keep.tile([P, N], BF16, name="bias")
 
-        def bias_to_columns():
-            bank = psum.tile([P, P], BF16, name="acc")
-            nc.tensor.transpose(bank[:], bias_rows[:], ident_bf[:])
-            columns = keep.tile([P, N // P], BF16, name="bias_columns")
-            nc.vector.tensor_copy(out=columns[:], in_=bank[:, : N // P])
+        def bias_to_columns(bank):
+            if bank is None:
+                bank = psum.tile([P, P], F32, name="turn")
+                nc.tensor.transpose(bank[:], bias_rows[:], ident[:])
+                return bank
+            columns = keep.tile([P, BIAS_ROWS], F32, name="bias_columns")
+            nc.vector.tensor_copy(out=columns[:], in_=bank[:, :BIAS_ROWS])
             return columns
 
         def spread_bias(columns):
-            bank = psum.tile([P, N], BF16, name="acc")
-            for c in range(N // P):
-                nc.tensor.transpose(bank[:, c * P : (c + 1) * P], columns[:, c : c + 1].to_broadcast([P, P]), ident_bf[:])
+            bank = psum.tile([P, BIAS_ROWS, P], F32, name="turn")
+            for c in range(BIAS_ROWS):
+                nc.tensor.transpose(bank[:, c, :], columns[:, c : c + 1].to_broadcast([P, P]), ident[:])
             return bank
 
         x_wide = {}
@@ -129,17 +144,17 @@ def tile_highway_gate_encode_b2_kernel(
         x_planes = {}
 
         def widen(pair, vector_blocks):
-            wide = work.tile([P, 2 * 512], BF16, name="x_wide", bufs=4)
+            wide = work.tile([P, 2 * 512], BF16, name="x_wide", bufs=10)
             for b in range(8):
                 i, j = divmod(8 * pair + b, K // B)
                 src = x_raw[i][:, j * B : (j + 1) * B].bitcast(FP8)
                 dst = wide[:, b * B : (b + 1) * B]
                 if b >= 8 - vector_blocks:
                     nc.vector.tensor_scalar(
-                        out=dst, in0=src, scalar1=x_scale[:, i, j : j + 1], scalar2=None, op0=ALU.mult
+                        out=dst, in0=src, scalar1=x_scale[i][:, j : j + 1], scalar2=None, op0=ALU.mult
                     )
                 else:
-                    nc.scalar.activation(out=dst, in_=src, func=ACT.Copy, scale=x_scale[:, i, j : j + 1])
+                    nc.scalar.activation(out=dst, in_=src, func=ACT.Copy, scale=x_scale[i][:, j : j + 1])
             x_wide[pair] = wide
 
         def turn_x(pair):
@@ -202,7 +217,7 @@ def tile_highway_gate_encode_b2_kernel(
 
         def sigmoid(i, halves):
             c = cols_of(halves)
-            nc.scalar.activation(out=f32_tile("gate", i)[:, c], in_=f32_tile("pre", i)[:, c], func=ACT.Sigmoid)
+            nc.scalar.activation(out=f32_tile("gate", i, 3)[:, c], in_=f32_tile("pre", i)[:, c], func=ACT.Sigmoid)
 
         def subtract(i, halves):
             c = cols_of(halves)
@@ -213,7 +228,7 @@ def tile_highway_gate_encode_b2_kernel(
         def gate_mult(i, halves):
             c = cols_of(halves)
             nc.vector.tensor_tensor(
-                out=f32_tile("step", i)[:, c], in0=f32_tile("gate", i)[:, c], in1=f32_tile("diff", i)[:, c], op=ALU.mult
+                out=f32_tile("step", i)[:, c], in0=f32_tile("gate", i, 3)[:, c], in1=f32_tile("diff", i)[:, c], op=ALU.mult
             )
 
         def add_carry(i, halves):
@@ -228,7 +243,7 @@ def tile_highway_gate_encode_b2_kernel(
 
         def round_y(i, halves):
             if i not in y_round:
-                y_round[i] = work.tile([P, N], BF16, name="y_round")
+                y_round[i] = work.tile([P, N], BF16, name="y_round", bufs=3)
             c = cols_of(halves)
             nc.scalar.copy(
                 out=y_round[i][:, c].rearrange("m (g u p e) -> m g u p e", u=2, p=P, e=2),
@@ -245,7 +260,7 @@ def tile_highway_gate_encode_b2_kernel(
 
         def empty_y(i, halves):
             if i not in y_grouped:
-                y_grouped[i] = work.tile([P, N], BF16, name="y_grouped", bufs=3, align_bytes=64)
+                y_grouped[i] = work.tile([P, N], BF16, name="y_grouped", bufs=4, align_bytes=64)
             nc.scalar.copy(
                 out=y_grouped[i][:, cols_of(halves)].bitcast(F32).rearrange("p (g r u) -> p g r u", r=P, u=2),
                 in_=y_bank[i, halves[0]][:].rearrange("p (g u) r -> p g r u", u=2),
@@ -253,104 +268,120 @@ def tile_highway_gate_encode_b2_kernel(
 
         y_codes = {}
         y_planes = {}
-        for first, last in STORE_BATCHES:
-            width = (last - first) * P
-            y_codes[first] = keep.tile([P, 2, width], U32, name="y_codes%d" % first, align_bytes=64)
-            y_planes[first] = keep.tile([P, 2, width], U8, name="y_plane%d" % first, align_bytes=64)
+        for first, end in SCALE_BATCHES:
+            y_planes[first] = keep.tile([P, 2, (end - first) * P], U8, name="y_plane%d" % first, align_bytes=64)
+        for first, end in CODE_BATCHES:
+            y_codes[first] = keep.tile([P, 2, (end - first) * P], U32, name="y_codes%d" % first, align_bytes=64)
+
+        def batch_of(batches, i):
+            return [b for b in batches if b[0] <= i < b[1]][0]
 
         def quantize_y(i, halves):
-            first, last = [b for b in STORE_BATCHES if b[0] <= i < b[1]][0]
-            cols = slice((i - first) * P, (i - first + 1) * P)
+            first, end = batch_of(CODE_BATCHES, i)
+            plane_first, plane_end = batch_of(SCALE_BATCHES, i)
             for g in halves:
                 nc.vector.quantize_mx(
-                    out=y_codes[first][:, g, cols].bitcast(FP8X4),
-                    scales=y_planes[first][:, g, cols],
+                    out=y_codes[first][:, g, (i - first) * P : (i - first + 1) * P].bitcast(FP8X4),
+                    scales=y_planes[plane_first][:, g, (i - plane_first) * P : (i - plane_first + 1) * P],
                     in_=y_grouped[i][:, cols_of([g])],
                 )
-            if i == last - 1:
-                tokens = slice(first * P, last * P)
-                groups = slice(halves[0], halves[-1] + 1)
+            if i == end - 1 and halves[-1] == 1:
                 nc.sync.dma_start(
-                    out=out_1[groups, :, tokens, :].rearrange("g p m t -> p g (m t)").bitcast(I32),
-                    in_=y_codes[first][:, groups, :].bitcast(I32),
+                    out=out_1[:, :, first * P : end * P, :].rearrange("g p m t -> p g (m t)").bitcast(I32),
+                    in_=y_codes[first][:].bitcast(I32),
                 )
-            if i == last - 1 and halves[-1] == 1:
-                for q in range(4):
-                    queue = nc.scalar if (last == TILES and q % 2 == 0) else nc.sync
-                    queue.dma_start(
-                        out=out_2[:, 4 * q : 4 * q + 4, tokens].rearrange("g r m -> r g m").bitcast(I32),
-                        in_=y_planes[first][32 * q : 32 * q + 4, :, :].bitcast(I32),
-                    )
+            if i == plane_end - 1 and halves[-1] == 1:
+                store_scales(plane_first, plane_end)
+
+        def store_scales(first, end):
+            for q in range(4):
+                queue = nc.scalar if (end == TILES and q % 2 == 0) else nc.sync
+                queue.dma_start(
+                    out=out_2[:, 4 * q : 4 * q + 4, first * P : end * P].rearrange("g r m -> r g m").bitcast(I32),
+                    in_=y_planes[first][32 * q : 32 * q + 4, :, :].bitcast(I32),
+                )
 
         both = [0, 1]
 
-        order = ((1, 0), (1, 1), (0, 0), (0, 1))
-        for s in range(HEAD_PAIRS):
-            widen(s, OPENING_VECTOR_BLOCKS if s < 2 else HEAD_VECTOR_BLOCKS)
-            if s == 2:
-                columns = bias_to_columns()
-            if s == 3:
-                spread = spread_bias(columns)
-            turn_x(s)
-            if s >= 1:
-                empty_x(s - 1)
-            if s >= 3:
-                quantize_x(s - 3)
-        nc.scalar.copy(out=bias[:], in_=spread[:])
-        for w, half in order:
-            multiply(0, w, half)
-        empty_x(HEAD_PAIRS - 1)
+        for pair in range(3):
+            widen(pair, 5)
+            turn_x(pair)
+        columns = bias_to_columns(None)
+        widen(3, 6)
+        empty_x(0)
+        quantize_x(0)
+        widen(4, 8)
+        empty_x(1)
+        quantize_x(1)
+        multiply(0, 1, 0)
+        columns = bias_to_columns(columns)
+        spread = spread_bias(columns)
+        empty_x(2)
+        widen(5, 5)
+        quantize_x(2)
+        multiply(0, 0, 0)
+        widen(6, 5)
+        nc.scalar.copy(out=bias[:].bitcast(F32), in_=spread[:].rearrange("p c j -> p (c j)"))
+        turn_x(3)
+        multiply(0, 1, 1)
+        multiply(0, 0, 1)
+        widen(7, 8)
 
         last = TILES - 1
-        waiting = list(range(HEAD_PAIRS, HEAD_PAIRS + FIRST_STEP_PAIRS))
-        quantize_x(HEAD_PAIRS - 3)
-        widen(waiting[0], 8)
-        quantize_x(HEAD_PAIRS - 2)
-        add_bias(0, 0)
-        quantize_x(HEAD_PAIRS - 1)
-        add_bias(0, 1)
-        widen(waiting[1], FIRST_VECTOR_BLOCKS)
-        widen(waiting[2], FIRST_VECTOR_BLOCKS)
-        tanh(0, 0)
-        tanh(0, 1)
-        for w, half in order:
-            multiply(1, w, half)
-        sigmoid(0, both)
-        subtract(0, both)
-        for s in range(1, TILES):
-            turned = waiting
-            waiting = [p for p in range(HEAD_PAIRS + FIRST_STEP_PAIRS, PAIRS) if p - PAIRS + LAST_WIDEN_STEP + 1 == s]
+        late = list(range(10, PAIRS))
+        for s in range(last):
+            turned = [p for p in range(4, PAIRS) if (2 * p) // 3 == s + 2]
+            add_bias(s, 0)
+            tanh(s, 0)
+            if s == 0:
+                empty_x(3)
+                widen(8, 4)
+                quantize_x(3)
+            else:
+                gate_mult(s - 1, both)
+            multiply(s + 1, 1, 0)
             for pair in turned:
                 turn_x(pair)
             if s >= 2:
                 turn_y(s - 2, both)
-            add_bias(s, 0)
-            gate_mult(s - 1, both)
+            multiply(s + 1, 0, 0)
             add_bias(s, 1)
-            tanh(s, 0)
             tanh(s, 1)
-            if s < last:
-                for w, half in order:
-                    multiply(s + 1, w, half)
+            multiply(s + 1, 1, 1)
+            multiply(s + 1, 0, 1)
+            sigmoid(s, both)
             for pair in turned:
                 empty_x(pair)
-            if s < last:
-                sigmoid(s, both)
+            if s == 0:
+                widen(9, 8)
             else:
-                sigmoid(s, [0])
-                sigmoid(s, [1])
-            add_carry(s - 1, both)
+                add_carry(s - 1, both)
+            subtract(s, both)
             if s >= 3:
                 quantize_y(s - 3, both)
+            if s >= 1:
+                round_y(s - 1, both)
             if s >= 2:
                 empty_y(s - 2, both)
-            subtract(s, both)
-            round_y(s - 1, both)
-            for pair in waiting:
-                widen(pair, LOOP_VECTOR_BLOCKS)
+            if s in WIDEN_STEPS:
+                widen(late.pop(0), LOOP_VECTOR_BLOCKS)
             for pair in turned:
                 quantize_x(pair)
-        quantize_y(last - 2, both)
+
+        gate_mult(last - 1, both)
+        add_bias(last, 0)
+        tanh(last, 0)
+        turn_y(last - 2, both)
+        add_carry(last - 1, both)
+        add_bias(last, 1)
+        tanh(last, 1)
+        empty_y(last - 2, both)
+        sigmoid(last, [0])
+        quantize_y(last - 3, both)
+        subtract(last, [0])
+        subtract(last, [1])
+        round_y(last - 1, both)
+        sigmoid(last, [1])
         turn_y(last - 1, both)
         gate_mult(last, [0])
         gate_mult(last, [1])
@@ -358,11 +389,16 @@ def tile_highway_gate_encode_b2_kernel(
         empty_y(last - 1, both)
         round_y(last, [0])
         turn_y(last, [0])
+        closing = work.tile([P, HALF], BF16, name="closing", bufs=1)
+        c = cols_of([1])
+        nc.vector.tensor_tensor(out=closing[:], in0=f32_tile("step", last)[:, c], in1=carry_sb[last][:, c], op=ALU.add)
+        bank = psum.tile([P, 2, P], F32, name="turn")
+        for u in range(2):
+            nc.tensor.transpose(bank[:, u, :], closing[:].bitcast(F32)[:, u::2], ident[:])
+        y_bank[last, 1] = bank
         add_carry(last, [1])
-        quantize_y(last - 1, both)
-        round_y(last, [1])
-        turn_y(last, [1])
         empty_y(last, [0])
         empty_y(last, [1])
-        quantize_y(last, [0])
-        quantize_y(last, [1])
+        quantize_y(last - 2, both)
+        quantize_y(last - 1, both)
+        quantize_y(last, both)

@@ -28,9 +28,11 @@ FIRST_VECTOR_BLOCKS = 4
 LAST_WIDEN_STEP = 6
 OPENING_VECTOR_BLOCKS = 5
 HEAD_VECTOR_BLOCKS = 7
-LOOP_VECTOR_BLOCKS = 2
-BIAS_ROWS = N // (2 * P)
-WIDEN_STEPS = (0, 1, 3, 5, 6)
+LOOP_VECTOR_BLOCKS = 0
+BIAS_WORDS = N // (2 * P)
+HEAD_TURNS = 5
+HEAD_WIDENS = 13
+POOL_COLUMNS = 384
 CODE_BATCHES = ((0, 4), (4, 7), (7, 9), (9, 10))
 SCALE_BATCHES = ((0, 7), (7, 10))
 
@@ -59,11 +61,8 @@ def tile_highway_gate_encode_b2_kernel(
                 x_scale[i] = tile[:, i - first, :]
 
         load_x_scale(0, 3, nc.scalar)
-        bias_rows = keep.tile([P, P], F32, name="bias_rows")
-        nc.vector.memset(bias_rows[:], 0.0)
-        nc.scalar.dma_start(
-            out=bias_rows[:BIAS_ROWS, :].bitcast(BF16), in_=b_gate.rearrange("o (c j) -> (o c) j", c=BIAS_ROWS)
-        )
+        bias_words = keep.tile([P, BIAS_WORDS], F32, name="bias_words")
+        nc.scalar.dma_start(out=bias_words[:].bitcast(BF16), in_=b_gate.rearrange("o (p j) -> (o p) j", p=P))
         warm = keep.tile([P, 1], F32, name="warm")
         nc.vector.memset(warm[:], 0.0)
         w_scales = []
@@ -105,37 +104,25 @@ def tile_highway_gate_encode_b2_kernel(
 
         load_x(0, 1)
         load_x(1, 3)
+        load_x_scale(3, TILES, nc.sync)
+        load_x(3, 6)
+        load_x(6, TILES)
         load_scales(1)
         load_words(1, 0)
-        load_x_scale(3, TILES, nc.sync)
-        load_x(3, 5)
         load_scales(0)
         load_words(0, 0)
-        load_x(5, 7)
         load_words(1, 1)
         load_words(0, 1)
         load_carry(0, 1)
-        load_x(7, TILES)
         load_carry(1, 2)
         load_carry(2, 6)
         load_carry(6, TILES)
 
         bias = keep.tile([P, N], BF16, name="bias")
 
-        def bias_to_columns(bank):
-            if bank is None:
-                bank = psum.tile([P, P], F32, name="turn")
-                nc.tensor.transpose(bank[:], bias_rows[:], ident[:])
-                return bank
-            columns = keep.tile([P, BIAS_ROWS], F32, name="bias_columns")
-            nc.vector.tensor_copy(out=columns[:], in_=bank[:, :BIAS_ROWS])
-            return columns
-
-        def spread_bias(columns):
-            bank = psum.tile([P, BIAS_ROWS, P], F32, name="turn")
-            for c in range(BIAS_ROWS):
-                nc.tensor.transpose(bank[:, c, :], columns[:, c : c + 1].to_broadcast([P, P]), ident[:])
-            return bank
+        spread = psum.tile([P, BIAS_WORDS, P], F32, name="turn")
+        for j in range(BIAS_WORDS):
+            nc.tensor.transpose(spread[:, j, :], bias_words[:, j : j + 1].to_broadcast([P, P]), ident[:])
 
         x_wide = {}
         x_bank = {}
@@ -144,7 +131,7 @@ def tile_highway_gate_encode_b2_kernel(
         x_planes = {}
 
         def widen(pair, vector_blocks):
-            wide = work.tile([P, 2 * 512], BF16, name="x_wide", bufs=10)
+            wide = work.tile([P, 2 * 512], BF16, name="x_wide", bufs=PAIRS)
             for b in range(8):
                 i, j = divmod(8 * pair + b, K // B)
                 src = x_raw[i][:, j * B : (j + 1) * B].bitcast(FP8)
@@ -183,7 +170,7 @@ def tile_highway_gate_encode_b2_kernel(
         acc = {}
 
         def multiply(i, w, half):
-            bank = psum.tile([P, HALF], F32, name="acc")
+            bank = psum.tile([P, HALF], F32, name="acc%d_%d" % (w, half), bufs=1)
             for g in range(PASSES):
                 pair, side = divmod(PASSES * i + g, 2)
                 cols = slice(side * P, (side + 1) * P)
@@ -219,16 +206,17 @@ def tile_highway_gate_encode_b2_kernel(
             c = cols_of(halves)
             nc.scalar.activation(out=f32_tile("gate", i, 3)[:, c], in_=f32_tile("pre", i)[:, c], func=ACT.Sigmoid)
 
-        def subtract(i, halves):
-            c = cols_of(halves)
-            nc.vector.tensor_tensor(
-                out=f32_tile("diff", i)[:, c], in0=f32_tile("cand", i)[:, c], in1=carry_sb[i][:, c], op=ALU.subtract
+        diff = {}
+
+        def subtract(engine, name, bufs, i, c):
+            diff[name, i] = work.tile([P, c.stop - c.start], F32, name=name, bufs=bufs)
+            engine.tensor_tensor(
+                out=diff[name, i][:], in0=f32_tile("cand", i)[:, c], in1=carry_sb[i][:, c], op=ALU.subtract
             )
 
-        def gate_mult(i, halves):
-            c = cols_of(halves)
+        def gate_mult(name, i, c):
             nc.vector.tensor_tensor(
-                out=f32_tile("step", i)[:, c], in0=f32_tile("gate", i, 3)[:, c], in1=f32_tile("diff", i)[:, c], op=ALU.mult
+                out=f32_tile("step", i)[:, c], in0=f32_tile("gate", i, 3)[:, c], in1=diff[name, i][:], op=ALU.mult
             )
 
         def add_carry(i, halves):
@@ -303,88 +291,82 @@ def tile_highway_gate_encode_b2_kernel(
 
         both = [0, 1]
 
-        for pair in range(3):
-            widen(pair, 5)
+        for pair in range(HEAD_TURNS):
+            widen(2 * pair, 5)
+            widen(2 * pair + 1, 6)
             turn_x(pair)
-        columns = bias_to_columns(None)
-        widen(3, 6)
-        empty_x(0)
-        quantize_x(0)
-        widen(4, 8)
-        empty_x(1)
-        quantize_x(1)
+            if pair == 0:
+                nc.scalar.copy(
+                    out=bias[:].bitcast(F32).rearrange("p (n j) -> p n j", j=BIAS_WORDS),
+                    in_=spread[:].rearrange("p j n -> p n j"),
+                )
+            if pair >= 1:
+                empty_x(pair - 1)
+            if pair >= 2:
+                quantize_x(pair - 2)
         multiply(0, 1, 0)
-        columns = bias_to_columns(columns)
-        spread = spread_bias(columns)
-        empty_x(2)
-        widen(5, 5)
-        quantize_x(2)
+        widen(2 * HEAD_TURNS, 6)
+        empty_x(HEAD_TURNS - 1)
+        quantize_x(HEAD_TURNS - 2)
+        for pair in range(2 * HEAD_TURNS + 1, HEAD_WIDENS):
+            widen(pair, 6)
+        quantize_x(HEAD_TURNS - 1)
         multiply(0, 0, 0)
-        widen(6, 5)
-        nc.scalar.copy(out=bias[:].bitcast(F32), in_=spread[:].rearrange("p c j -> p (c j)"))
-        turn_x(3)
+        tanh(0, 0)
         multiply(0, 1, 1)
         multiply(0, 0, 1)
-        widen(7, 8)
 
         last = TILES - 1
-        late = list(range(10, PAIRS))
-        for s in range(last):
-            turned = [p for p in range(4, PAIRS) if (2 * p) // 3 == s + 2]
+        low = slice(0, POOL_COLUMNS)
+        high = slice(POOL_COLUMNS, N)
+        for s in range(TILES):
+            turned = [p for p in range(HEAD_TURNS, PAIRS) if (2 * p) // 3 == s + 2]
+            if s >= 1:
+                gate_mult("diff_low", s - 1, low)
+                gate_mult("diff_high", s - 1, high)
+                subtract(nc.gpsimd, "diff_low", 1, s, low)
             add_bias(s, 0)
-            tanh(s, 0)
             if s == 0:
-                empty_x(3)
-                widen(8, 4)
-                quantize_x(3)
-            else:
-                gate_mult(s - 1, both)
-            multiply(s + 1, 1, 0)
+                widen(PAIRS - 2, 8)
+                widen(PAIRS - 1, 8)
+            add_bias(s, 1)
+            if s == 0:
+                subtract(nc.vector, "diff_low", 1, s, low)
+            tanh(s, 1)
+            if s < last:
+                multiply(s + 1, 0, 0)
             for pair in turned:
                 turn_x(pair)
             if s >= 2:
                 turn_y(s - 2, both)
-            multiply(s + 1, 0, 0)
-            add_bias(s, 1)
-            tanh(s, 1)
-            multiply(s + 1, 1, 1)
-            multiply(s + 1, 0, 1)
-            sigmoid(s, both)
+            if s < last:
+                multiply(s + 1, 1, 0)
+                multiply(s + 1, 1, 1)
+                multiply(s + 1, 0, 1)
+            if s == 0:
+                sigmoid(s, both)
+            if s < last:
+                tanh(s + 1, 0)
+            if s >= 1:
+                sigmoid(s, both)
             for pair in turned:
                 empty_x(pair)
-            if s == 0:
-                widen(9, 8)
-            else:
+            if s >= 1:
                 add_carry(s - 1, both)
-            subtract(s, both)
+            subtract(nc.vector, "diff_high", 2, s, high)
             if s >= 3:
                 quantize_y(s - 3, both)
             if s >= 1:
                 round_y(s - 1, both)
             if s >= 2:
                 empty_y(s - 2, both)
-            if s in WIDEN_STEPS:
-                widen(late.pop(0), LOOP_VECTOR_BLOCKS)
             for pair in turned:
                 quantize_x(pair)
 
-        gate_mult(last - 1, both)
-        add_bias(last, 0)
-        tanh(last, 0)
-        turn_y(last - 2, both)
-        add_carry(last - 1, both)
-        add_bias(last, 1)
-        tanh(last, 1)
-        empty_y(last - 2, both)
-        sigmoid(last, [0])
-        quantize_y(last - 3, both)
-        subtract(last, [0])
-        subtract(last, [1])
-        round_y(last - 1, both)
-        sigmoid(last, [1])
         turn_y(last - 1, both)
-        gate_mult(last, [0])
-        gate_mult(last, [1])
+        gate_mult("diff_low", last, low)
+        gate_mult("diff_high", last, high)
+        quantize_y(last - 2, both)
         add_carry(last, [0])
         empty_y(last - 1, both)
         round_y(last, [0])
@@ -399,6 +381,5 @@ def tile_highway_gate_encode_b2_kernel(
         add_carry(last, [1])
         empty_y(last, [0])
         empty_y(last, [1])
-        quantize_y(last - 2, both)
         quantize_y(last - 1, both)
         quantize_y(last, both)

@@ -32,9 +32,8 @@ LOOP_VECTOR_BLOCKS = 0
 BIAS_WORDS = N // (2 * P)
 HEAD_TURNS = 5
 HEAD_WIDENS = 13
-POOL_COLUMNS = 384
-CODE_BATCHES = ((0, 4), (4, 7), (7, 9), (9, 10))
-SCALE_BATCHES = ((0, 7), (7, 10))
+POOL_COLUMNS = 512
+PLANE_BATCHES = ((0, 2), (2, 4), (4, 6), (6, 8), (8, 10))
 
 
 def tile_highway_gate_encode_b2_kernel(
@@ -152,20 +151,23 @@ def tile_highway_gate_encode_b2_kernel(
                 nc.tensor.transpose(bank[:, s, :], words[:, 256 * g + u : 256 * (g + 1) : 2], ident[:])
             x_bank[pair] = bank
 
-        def empty_x(pair):
-            grouped = work.tile([P, 2 * 512], BF16, name="x_grouped", bufs=4, align_bytes=64)
-            nc.scalar.copy(
-                out=grouped[:].bitcast(F32).rearrange("p (g r u) -> p g r u", g=2, u=2),
-                in_=x_bank[pair][:].rearrange("p (g u) r -> p g r u", u=2),
-            )
-            x_grouped[pair] = grouped
+        def empty_x(pairs):
+            grouped = work.tile([P, len(pairs) * 1024], BF16, name="x_grouped", bufs=3, align_bytes=64)
+            for n, pair in enumerate(pairs):
+                nc.scalar.copy(
+                    out=grouped[:, n * 1024 : (n + 1) * 1024].bitcast(F32).rearrange("p (g r u) -> p g r u", g=2, u=2),
+                    in_=x_bank[pair][:].rearrange("p (g u) r -> p g r u", u=2),
+                )
+            x_grouped[pairs[0]] = grouped
 
-        def quantize_x(pair):
-            codes = keep.tile([P, 2 * P], U32, name="x_codes%d" % pair, align_bytes=64)
-            plane = keep.tile([P, 2 * P], U8, name="x_plane%d" % pair, align_bytes=64)
-            nc.vector.quantize_mx(out=codes[:].bitcast(FP8X4), scales=plane[:], in_=x_grouped[pair][:])
-            x_codes[pair] = codes
-            x_planes[pair] = plane
+        def quantize_x(pairs):
+            width = len(pairs) * 2 * P
+            codes = keep.tile([P, width], U32, name="x_codes%d" % pairs[0], align_bytes=64)
+            plane = keep.tile([P, width], U8, name="x_plane%d" % pairs[0], align_bytes=64)
+            nc.vector.quantize_mx(out=codes[:].bitcast(FP8X4), scales=plane[:], in_=x_grouped[pairs[0]][:])
+            for n, pair in enumerate(pairs):
+                x_codes[pair] = codes[:, n * 2 * P : (n + 1) * 2 * P]
+                x_planes[pair] = plane[:, n * 2 * P : (n + 1) * 2 * P]
 
         acc = {}
 
@@ -247,47 +249,40 @@ def tile_highway_gate_encode_b2_kernel(
             y_bank[i, halves[0]] = bank
 
         def empty_y(i, halves):
-            if i not in y_grouped:
-                y_grouped[i] = work.tile([P, N], BF16, name="y_grouped", bufs=4, align_bytes=64)
+            first, end = [b for b in PLANE_BATCHES if b[0] <= i < b[1]][0]
+            if first not in y_grouped:
+                y_grouped[first] = keep.tile([P, 2, (end - first) * HALF], BF16, name="y_grouped%d" % first, align_bytes=64)
+            dst = y_grouped[first][:, halves[0] : halves[-1] + 1, (i - first) * HALF : (i - first + 1) * HALF]
             nc.scalar.copy(
-                out=y_grouped[i][:, cols_of(halves)].bitcast(F32).rearrange("p (g r u) -> p g r u", r=P, u=2),
+                out=dst.bitcast(F32).rearrange("p g (r u) -> p g r u", u=2),
                 in_=y_bank[i, halves[0]][:].rearrange("p (g u) r -> p g r u", u=2),
             )
 
-        y_codes = {}
         y_planes = {}
-        for first, end in SCALE_BATCHES:
-            y_planes[first] = keep.tile([P, 2, (end - first) * P], U8, name="y_plane%d" % first, align_bytes=64)
-        for first, end in CODE_BATCHES:
-            y_codes[first] = keep.tile([P, 2, (end - first) * P], U32, name="y_codes%d" % first, align_bytes=64)
 
-        def batch_of(batches, i):
-            return [b for b in batches if b[0] <= i < b[1]][0]
-
-        def quantize_y(i, halves):
-            first, end = batch_of(CODE_BATCHES, i)
-            plane_first, plane_end = batch_of(SCALE_BATCHES, i)
-            for g in halves:
-                nc.vector.quantize_mx(
-                    out=y_codes[first][:, g, (i - first) * P : (i - first + 1) * P].bitcast(FP8X4),
-                    scales=y_planes[plane_first][:, g, (i - plane_first) * P : (i - plane_first + 1) * P],
-                    in_=y_grouped[i][:, cols_of([g])],
-                )
-            if i == end - 1 and halves[-1] == 1:
-                nc.sync.dma_start(
-                    out=out_1[:, :, first * P : end * P, :].rearrange("g p m t -> p g (m t)").bitcast(I32),
-                    in_=y_codes[first][:].bitcast(I32),
-                )
-            if i == plane_end - 1 and halves[-1] == 1:
-                store_scales(plane_first, plane_end)
-
-        def store_scales(first, end):
-            for q in range(4):
-                queue = nc.scalar if (end == TILES and q % 2 == 0) else nc.sync
-                queue.dma_start(
-                    out=out_2[:, 4 * q : 4 * q + 4, first * P : end * P].rearrange("g r m -> r g m").bitcast(I32),
-                    in_=y_planes[first][32 * q : 32 * q + 4, :, :].bitcast(I32),
-                )
+        def quantize_y(batch, halves):
+            first, end = batch
+            tokens = slice(first * P, end * P)
+            width = (end - first) * P
+            groups = slice(halves[0], halves[-1] + 1)
+            codes = keep.tile([P, len(halves), width], U32, name="y_codes%d_%d" % (first, halves[0]), align_bytes=64)
+            if first not in y_planes:
+                y_planes[first] = keep.tile([P, 2, width], U8, name="y_plane%d" % first, align_bytes=64)
+            nc.vector.quantize_mx(
+                out=codes[:].rearrange("p g m -> p (g m)").bitcast(FP8X4),
+                scales=y_planes[first][:, groups, :].rearrange("p g m -> p (g m)"),
+                in_=y_grouped[first][:, groups, :].rearrange("p g c -> p (g c)"),
+            )
+            nc.sync.dma_start(
+                out=out_1[groups, :, tokens, :].rearrange("g p m t -> p g (m t)").bitcast(I32), in_=codes[:].bitcast(I32)
+            )
+            if halves[-1] == 1:
+                for q in range(4):
+                    queue = nc.scalar if (tokens.stop == T and q % 2 == 0) else nc.sync
+                    queue.dma_start(
+                        out=out_2[:, 4 * q : 4 * q + 4, tokens].rearrange("g r m -> r g m").bitcast(I32),
+                        in_=y_planes[first][32 * q : 32 * q + 4, :, :].bitcast(I32),
+                    )
 
         both = [0, 1]
 
@@ -301,16 +296,16 @@ def tile_highway_gate_encode_b2_kernel(
                     in_=spread[:].rearrange("p j n -> p n j"),
                 )
             if pair >= 1:
-                empty_x(pair - 1)
+                empty_x([pair - 1])
             if pair >= 2:
-                quantize_x(pair - 2)
+                quantize_x([pair - 2])
         multiply(0, 1, 0)
         widen(2 * HEAD_TURNS, 6)
-        empty_x(HEAD_TURNS - 1)
-        quantize_x(HEAD_TURNS - 2)
+        empty_x([HEAD_TURNS - 1])
+        quantize_x([HEAD_TURNS - 2])
         for pair in range(2 * HEAD_TURNS + 1, HEAD_WIDENS):
             widen(pair, 6)
-        quantize_x(HEAD_TURNS - 1)
+        quantize_x([HEAD_TURNS - 1])
         multiply(0, 0, 0)
         tanh(0, 0)
         multiply(0, 1, 1)
@@ -319,16 +314,18 @@ def tile_highway_gate_encode_b2_kernel(
         last = TILES - 1
         low = slice(0, POOL_COLUMNS)
         high = slice(POOL_COLUMNS, N)
+        turned = []
         for s in range(TILES):
-            turned = [p for p in range(HEAD_TURNS, PAIRS) if (2 * p) // 3 == s + 2]
+            emptied = turned
+            turned = [p for p in range(HEAD_TURNS, PAIRS) if (2 * p) // 3 == s + 3]
             if s >= 1:
                 gate_mult("diff_low", s - 1, low)
                 gate_mult("diff_high", s - 1, high)
                 subtract(nc.gpsimd, "diff_low", 1, s, low)
             add_bias(s, 0)
             if s == 0:
+                sigmoid(s, [0])
                 widen(PAIRS - 2, 8)
-                widen(PAIRS - 1, 8)
             add_bias(s, 1)
             if s == 0:
                 subtract(nc.vector, "diff_low", 1, s, low)
@@ -344,29 +341,34 @@ def tile_highway_gate_encode_b2_kernel(
                 multiply(s + 1, 1, 1)
                 multiply(s + 1, 0, 1)
             if s == 0:
-                sigmoid(s, both)
+                sigmoid(s, [1])
             if s < last:
                 tanh(s + 1, 0)
+            if s == last:
+                empty_y(s - 2, both)
             if s >= 1:
                 sigmoid(s, both)
-            for pair in turned:
-                empty_x(pair)
+            if turned:
+                empty_x(turned)
+            if s == 0:
+                widen(PAIRS - 1, 0)
             if s >= 1:
                 add_carry(s - 1, both)
             subtract(nc.vector, "diff_high", 2, s, high)
-            if s >= 3:
-                quantize_y(s - 3, both)
+            if s >= 4 and s % 2 == 0:
+                quantize_y(PLANE_BATCHES[(s - 4) // 2], both)
+            if s == last:
+                quantize_y(PLANE_BATCHES[-2], both)
             if s >= 1:
                 round_y(s - 1, both)
-            if s >= 2:
+            if 2 <= s < last:
                 empty_y(s - 2, both)
-            for pair in turned:
-                quantize_x(pair)
+            if emptied:
+                quantize_x(emptied)
 
         turn_y(last - 1, both)
         gate_mult("diff_low", last, low)
         gate_mult("diff_high", last, high)
-        quantize_y(last - 2, both)
         add_carry(last, [0])
         empty_y(last - 1, both)
         round_y(last, [0])
@@ -381,5 +383,5 @@ def tile_highway_gate_encode_b2_kernel(
         add_carry(last, [1])
         empty_y(last, [0])
         empty_y(last, [1])
-        quantize_y(last - 1, both)
-        quantize_y(last, both)
+        quantize_y(PLANE_BATCHES[-1], [0])
+        quantize_y(PLANE_BATCHES[-1], [1])

@@ -30,9 +30,10 @@ OPENING_VECTOR_BLOCKS = 5
 HEAD_VECTOR_BLOCKS = 7
 LOOP_VECTOR_BLOCKS = 0
 BIAS_WORDS = N // (2 * P)
-HEAD_TURNS = 5
+HEAD_TURNS = 6
+SORTED_PAIRS = range(5, 13)
 HEAD_WIDENS = 13
-POOL_COLUMNS = 512
+POOL_COLUMNS = 416
 PLANE_BATCHES = ((0, 2), (2, 4), (4, 6), (6, 8), (8, 10))
 
 
@@ -105,11 +106,11 @@ def tile_highway_gate_encode_b2_kernel(
         load_x(1, 3)
         load_x_scale(3, TILES, nc.sync)
         load_x(3, 6)
-        load_x(6, TILES)
         load_scales(1)
         load_words(1, 0)
         load_scales(0)
         load_words(0, 0)
+        load_x(6, TILES)
         load_words(1, 1)
         load_words(0, 1)
         load_carry(0, 1)
@@ -135,6 +136,11 @@ def tile_highway_gate_encode_b2_kernel(
                 i, j = divmod(8 * pair + b, K // B)
                 src = x_raw[i][:, j * B : (j + 1) * B].bitcast(FP8)
                 dst = wide[:, b * B : (b + 1) * B]
+                if pair in SORTED_PAIRS:
+                    g, q = divmod(b, 4)
+                    src = src.rearrange("m (p u e) -> m p u e", u=2, e=2)
+                    dst = wide[:, g * 512 : (g + 1) * 512].rearrange("m (u p e) -> m p u e", u=2, e=2)
+                    dst = dst[:, 32 * q : 32 * (q + 1), :, :]
                 if b >= 8 - vector_blocks:
                     nc.vector.tensor_scalar(
                         out=dst, in0=src, scalar1=x_scale[i][:, j : j + 1], scalar2=None, op0=ALU.mult
@@ -148,7 +154,11 @@ def tile_highway_gate_encode_b2_kernel(
             bank = psum.tile([P, 4, P], F32, name="turn")
             for s in range(4):
                 g, u = divmod(s, 2)
-                nc.tensor.transpose(bank[:, s, :], words[:, 256 * g + u : 256 * (g + 1) : 2], ident[:])
+                if pair in SORTED_PAIRS:
+                    src = words[:, s * P : (s + 1) * P]
+                else:
+                    src = words[:, 256 * g + u : 256 * (g + 1) : 2]
+                nc.tensor.transpose(bank[:, s, :], src, ident[:])
             x_bank[pair] = bank
 
         def empty_x(pairs):
@@ -286,30 +296,43 @@ def tile_highway_gate_encode_b2_kernel(
 
         both = [0, 1]
 
-        for pair in range(HEAD_TURNS):
-            widen(2 * pair, 5)
-            widen(2 * pair + 1, 6)
-            turn_x(pair)
-            if pair == 0:
-                nc.scalar.copy(
-                    out=bias[:].bitcast(F32).rearrange("p (n j) -> p n j", j=BIAS_WORDS),
-                    in_=spread[:].rearrange("p j n -> p n j"),
-                )
-            if pair >= 1:
-                empty_x([pair - 1])
-            if pair >= 2:
-                quantize_x([pair - 2])
+        widen(0, 5)
+        turn_x(0)
+        widen(1, 5)
+        turn_x(1)
+        nc.scalar.copy(
+            out=bias[:].bitcast(F32).rearrange("p (n j) -> p n j", j=BIAS_WORDS), in_=spread[:].rearrange("p j n -> p n j")
+        )
+        widen(2, 8)
+        turn_x(2)
+        empty_x([0])
+        widen(5, 8)
+        quantize_x([0])
+        empty_x([1])
+        widen(6, 8)
+        quantize_x([1])
         multiply(0, 1, 0)
-        widen(2 * HEAD_TURNS, 6)
-        empty_x([HEAD_TURNS - 1])
-        quantize_x([HEAD_TURNS - 2])
-        for pair in range(2 * HEAD_TURNS + 1, HEAD_WIDENS):
-            widen(pair, 6)
-        quantize_x([HEAD_TURNS - 1])
+        widen(3, 0)
+        empty_x([2])
+        turn_x(3)
+        widen(7, 8)
+        widen(8, 8)
+        quantize_x([2])
+        widen(4, 0)
         multiply(0, 0, 0)
+        turn_x(4)
+        turn_x(5)
+        add_bias(0, 0)
+        empty_x([3])
         tanh(0, 0)
+        sigmoid(0, [0])
+        empty_x([4, 5])
+        widen(9, 8)
+        quantize_x([3])
+        widen(10, 8)
         multiply(0, 1, 1)
         multiply(0, 0, 1)
+        widen(11, 8)
 
         last = TILES - 1
         low = slice(0, POOL_COLUMNS)
@@ -322,13 +345,12 @@ def tile_highway_gate_encode_b2_kernel(
                 gate_mult("diff_low", s - 1, low)
                 gate_mult("diff_high", s - 1, high)
                 subtract(nc.gpsimd, "diff_low", 1, s, low)
-            add_bias(s, 0)
-            if s == 0:
-                sigmoid(s, [0])
-                widen(PAIRS - 2, 8)
+                add_bias(s, 0)
             add_bias(s, 1)
             if s == 0:
+                widen(12, 8)
                 subtract(nc.vector, "diff_low", 1, s, low)
+                quantize_x([4, 5])
             tanh(s, 1)
             if s < last:
                 multiply(s + 1, 0, 0)
@@ -351,14 +373,13 @@ def tile_highway_gate_encode_b2_kernel(
             if turned:
                 empty_x(turned)
             if s == 0:
+                widen(PAIRS - 2, 0)
                 widen(PAIRS - 1, 0)
             if s >= 1:
                 add_carry(s - 1, both)
             subtract(nc.vector, "diff_high", 2, s, high)
             if s >= 4 and s % 2 == 0:
                 quantize_y(PLANE_BATCHES[(s - 4) // 2], both)
-            if s == last:
-                quantize_y(PLANE_BATCHES[-2], both)
             if s >= 1:
                 round_y(s - 1, both)
             if 2 <= s < last:
@@ -369,6 +390,7 @@ def tile_highway_gate_encode_b2_kernel(
         turn_y(last - 1, both)
         gate_mult("diff_low", last, low)
         gate_mult("diff_high", last, high)
+        quantize_y(PLANE_BATCHES[-2], both)
         add_carry(last, [0])
         empty_y(last - 1, both)
         round_y(last, [0])

from contextlib import ExitStack

import concourse.mybir as mybir
from concourse.masks import make_identity

T, K, N, B = 1280, 1536, 1024, 128
FLOPS = 2 * 2 * T * K * N

F32 = mybir.dt.float32
BF16 = mybir.dt.bfloat16
I32 = mybir.dt.int32
U32 = mybir.dt.uint32
U8 = mybir.dt.uint8
FP8 = mybir.dt.float8_e4m3fn
FP8X4 = mybir.dt.float8_e4m3fn_x4
FP4X4 = mybir.dt.float4_e2m1fn_x4
ALU = mybir.AluOpType
ACT = mybir.ActivationFunctionType

P = 128
TILES = T // P
PASSES = K // 512
HALF = 512
PAIRS = TILES * PASSES // 2
HEAD_PAIRS = 7
FIRST_STEP_PAIRS = 3
FIRST_VECTOR_BLOCKS = 4
LAST_WIDEN_STEP = 6
OPENING_VECTOR_BLOCKS = 5
HEAD_VECTOR_BLOCKS = 7
LOOP_VECTOR_BLOCKS = 0
BIAS_WORDS = N // (2 * P)
HEAD_TURNS = 6
SORTED_PAIRS = range(5, 13)
HEAD_WIDENS = 13
POOL_COLUMNS = 416
PLANE_BATCHES = ((0, 2), (2, 4), (4, 6), (6, 8), (8, 10))


def tile_highway_gate_encode_b2_kernel(
    tc, X_bytes, X_scale, Wh_words, Wh_scales, Wg_words, Wg_scales, b_gate, carry, out_0, out_1, out_2
):
    nc = tc.nc
    with ExitStack() as ctx:
        keep = ctx.enter_context(tc.tile_pool(name="keep", bufs=1))
        work = ctx.enter_context(tc.tile_pool(name="work", bufs=2))
        psum = ctx.enter_context(tc.psum_pool(name="psum", bufs=4))
        ctx.enter_context(tc.manual_schedule())

        ident = keep.tile([P, P], F32, name="ident")
        make_identity(nc, ident[:])

        x_scale = {}

        def load_x_scale(first, last, queue):
            tile = keep.tile([P, last - first, 16], F32, name="x_scale%d" % first)
            queue.dma_start(
                out=tile[:, :, : K // B], in_=X_scale[first * P : last * P, :].rearrange("(i p) j -> p i j", p=P)
            )
            for i in range(first, last):
                x_scale[i] = tile[:, i - first, :]

        load_x_scale(0, 3, nc.scalar)
        bias_words = keep.tile([P, BIAS_WORDS], F32, name="bias_words")
        nc.scalar.dma_start(out=bias_words[:].bitcast(BF16), in_=b_gate.rearrange("o (p j) -> (o p) j", p=P))
        warm = keep.tile([P, 1], F32, name="warm")
        nc.vector.memset(warm[:], 0.0)
        w_scales = []
        for name in ("wg_scales", "wh_scales"):
            plane = keep.tile([P, PASSES, N], U8, name=name, align_bytes=64)
            nc.vector.memset(plane[:].bitcast(U32), 0)
            w_scales.insert(0, plane)
        nc.scalar.activation(out=warm[:], in_=warm[:], func=ACT.Sigmoid)

        x_raw = {}
        carry_sb = {}
        w_words = {}

        def load_x(first, last):
            raw = keep.tile([P, last - first, K], U8, name="x_raw%d" % first)
            nc.sync.dma_start(out=raw[:], in_=X_bytes[first * P : last * P, :].rearrange("(i p) k -> p i k", p=P))
            for i in range(first, last):
                x_raw[i] = raw[:, i - first, :]

        def load_carry(first, last):
            tile = keep.tile([P, last - first, N], BF16, name="carry%d" % first)
            nc.sync.dma_start(out=tile[:], in_=carry[first * P : last * P, :].rearrange("(i p) n -> p i n", p=P))
            for i in range(first, last):
                carry_sb[i] = tile[:, i - first, :]

        def load_words(w, half):
            tile = keep.tile([P, PASSES, 2 * HALF], U8, name="words%d_%d" % (w, half), align_bytes=64)
            src = (Wh_words, Wg_words)[w][:, :, half * 2 * HALF : (half + 1) * 2 * HALF]
            nc.sync.dma_start(out=tile[:].bitcast(I32), in_=src.rearrange("g p b -> p g b").bitcast(I32))
            w_words[w, half] = tile

        def load_scales(w):
            for q in range(4):
                src = (Wh_scales, Wg_scales)[w][:, 4 * q : 4 * q + 4, :]
                nc.sync.dma_start(
                    out=w_scales[w][32 * q : 32 * q + 4, :, :].bitcast(I32),
                    in_=src.rearrange("g r n -> r g n").bitcast(I32),
                )

        load_x(0, 1)
        load_x(1, 3)
        load_x_scale(3, TILES, nc.sync)
        load_x(3, 6)
        load_scales(1)
        load_words(1, 0)
        load_scales(0)
        load_words(0, 0)
        load_x(6, TILES)
        load_words(1, 1)
        load_words(0, 1)
        load_carry(0, 1)
        load_carry(1, 2)
        load_carry(2, 6)
        load_carry(6, TILES)

        bias = keep.tile([P, N], BF16, name="bias")

        spread = psum.tile([P, BIAS_WORDS, P], F32, name="turn")
        for j in range(BIAS_WORDS):
            nc.tensor.transpose(spread[:, j, :], bias_words[:, j : j + 1].to_broadcast([P, P]), ident[:])

        x_wide = {}
        x_bank = {}
        x_grouped = {}
        x_codes = {}
        x_planes = {}

        def widen(pair, vector_blocks):
            wide = work.tile([P, 2 * 512], BF16, name="x_wide", bufs=PAIRS)
            for b in range(8):
                i, j = divmod(8 * pair + b, K // B)
                src = x_raw[i][:, j * B : (j + 1) * B].bitcast(FP8)
                dst = wide[:, b * B : (b + 1) * B]
                if pair in SORTED_PAIRS:
                    g, q = divmod(b, 4)
                    src = src.rearrange("m (p u e) -> m p u e", u=2, e=2)
                    dst = wide[:, g * 512 : (g + 1) * 512].rearrange("m (u p e) -> m p u e", u=2, e=2)
                    dst = dst[:, 32 * q : 32 * (q + 1), :, :]
                if b >= 8 - vector_blocks:
                    nc.vector.tensor_scalar(
                        out=dst, in0=src, scalar1=x_scale[i][:, j : j + 1], scalar2=None, op0=ALU.mult
                    )
                else:
                    nc.scalar.activation(out=dst, in_=src, func=ACT.Copy, scale=x_scale[i][:, j : j + 1])
            x_wide[pair] = wide

        def turn_x(pair):
            words = x_wide[pair][:].bitcast(F32)
            bank = psum.tile([P, 4, P], F32, name="turn")
            for s in range(4):
                g, u = divmod(s, 2)
                if pair in SORTED_PAIRS:
                    src = words[:, s * P : (s + 1) * P]
                else:
                    src = words[:, 256 * g + u : 256 * (g + 1) : 2]
                nc.tensor.transpose(bank[:, s, :], src, ident[:])
            x_bank[pair] = bank

        def empty_x(pairs):
            grouped = work.tile([P, len(pairs) * 1024], BF16, name="x_grouped", bufs=3, align_bytes=64)
            for n, pair in enumerate(pairs):
                nc.scalar.copy(
                    out=grouped[:, n * 1024 : (n + 1) * 1024].bitcast(F32).rearrange("p (g r u) -> p g r u", g=2, u=2),
                    in_=x_bank[pair][:].rearrange("p (g u) r -> p g r u", u=2),
                )
            x_grouped[pairs[0]] = grouped

        def quantize_x(pairs):
            width = len(pairs) * 2 * P
            codes = keep.tile([P, width], U32, name="x_codes%d" % pairs[0], align_bytes=64)
            plane = keep.tile([P, width], U8, name="x_plane%d" % pairs[0], align_bytes=64)
            nc.vector.quantize_mx(out=codes[:].bitcast(FP8X4), scales=plane[:], in_=x_grouped[pairs[0]][:])
            for n, pair in enumerate(pairs):
                x_codes[pair] = codes[:, n * 2 * P : (n + 1) * 2 * P]
                x_planes[pair] = plane[:, n * 2 * P : (n + 1) * 2 * P]

        acc = {}

        def multiply(i, w, half):
            bank = psum.tile([P, HALF], F32, name="acc%d_%d" % (w, half), bufs=1)
            for g in range(PASSES):
                pair, side = divmod(PASSES * i + g, 2)
                cols = slice(side * P, (side + 1) * P)
                nc.tensor.matmul_mx(
                    out=bank[:],
                    lhsT=x_codes[pair][:, cols].bitcast(FP8X4),
                    lhsT_scale=x_planes[pair][:, cols],
                    rhs=w_words[w, half][:, g, :].bitcast(FP4X4),
                    rhs_scale=w_scales[w][:, g, half * HALF : (half + 1) * HALF],
                    start=(g == 0),
                    stop=(g == PASSES - 1),
                )
            acc[i, w, half] = bank

        tiles = {}

        def f32_tile(name, i, bufs=2):
            if (name, i) not in tiles:
                tiles[name, i] = work.tile([P, N], F32, name=name, bufs=bufs)
            return tiles[name, i]

        def cols_of(halves):
            return slice(halves[0] * HALF, (halves[-1] + 1) * HALF)

        def tanh(i, half):
            nc.scalar.activation(out=f32_tile("cand", i)[:, cols_of([half])], in_=acc[i, 0, half][:], func=ACT.Tanh)

        def add_bias(i, half):
            c = cols_of([half])
            nc.vector.tensor_tensor(out=f32_tile("pre", i)[:, c], in0=acc[i, 1, half][:], in1=bias[:, c], op=ALU.add)

        def sigmoid(i, halves):
            c = cols_of(halves)
            nc.scalar.activation(out=f32_tile("gate", i, 3)[:, c], in_=f32_tile("pre", i)[:, c], func=ACT.Sigmoid)

        diff = {}

        def subtract(engine, name, bufs, i, c):
            diff[name, i] = work.tile([P, c.stop - c.start], F32, name=name, bufs=bufs)
            engine.tensor_tensor(
                out=diff[name, i][:], in0=f32_tile("cand", i)[:, c], in1=carry_sb[i][:, c], op=ALU.subtract
            )

        def gate_mult(name, i, c):
            nc.vector.tensor_tensor(
                out=f32_tile("step", i)[:, c], in0=f32_tile("gate", i, 3)[:, c], in1=diff[name, i][:], op=ALU.mult
            )

        def add_carry(i, halves):
            c = cols_of(halves)
            y = f32_tile("y", i, 3)
            nc.vector.tensor_tensor(out=y[:, c], in0=f32_tile("step", i)[:, c], in1=carry_sb[i][:, c], op=ALU.add)
            nc.sync.dma_start(out=out_0[i * P : (i + 1) * P, c], in_=y[:, c])

        y_round = {}
        y_bank = {}
        y_grouped = {}

        def round_y(i, halves):
            if i not in y_round:
                y_round[i] = work.tile([P, N], BF16, name="y_round", bufs=3)
            c = cols_of(halves)
            nc.scalar.copy(
                out=y_round[i][:, c].rearrange("m (g u p e) -> m g u p e", u=2, p=P, e=2),
                in_=f32_tile("y", i, 3)[:, c].rearrange("m (g p u e) -> m g u p e", u=2, p=P, e=2),
            )

        def turn_y(i, halves):
            words = y_round[i][:].bitcast(F32)
            bank = psum.tile([P, 2 * len(halves), P], F32, name="turn")
            for s in range(2 * len(halves)):
                first = (2 * halves[0] + s) * P
                nc.tensor.transpose(bank[:, s, :], words[:, first : first + P], ident[:])
            y_bank[i, halves[0]] = bank

        def empty_y(i, halves):
            first, end = [b for b in PLANE_BATCHES if b[0] <= i < b[1]][0]
            if first not in y_grouped:
                y_grouped[first] = keep.tile([P, 2, (end - first) * HALF], BF16, name="y_grouped%d" % first, align_bytes=64)
            dst = y_grouped[first][:, halves[0] : halves[-1] + 1, (i - first) * HALF : (i - first + 1) * HALF]
            nc.scalar.copy(
                out=dst.bitcast(F32).rearrange("p g (r u) -> p g r u", u=2),
                in_=y_bank[i, halves[0]][:].rearrange("p (g u) r -> p g r u", u=2),
            )

        y_planes = {}

        def quantize_y(batch, halves):
            first, end = batch
            tokens = slice(first * P, end * P)
            width = (end - first) * P
            groups = slice(halves[0], halves[-1] + 1)
            codes = keep.tile([P, len(halves), width], U32, name="y_codes%d_%d" % (first, halves[0]), align_bytes=64)
            if first not in y_planes:
                y_planes[first] = keep.tile([P, 2, width], U8, name="y_plane%d" % first, align_bytes=64)
            nc.vector.quantize_mx(
                out=codes[:].rearrange("p g m -> p (g m)").bitcast(FP8X4),
                scales=y_planes[first][:, groups, :].rearrange("p g m -> p (g m)"),
                in_=y_grouped[first][:, groups, :].rearrange("p g c -> p (g c)"),
            )
            nc.sync.dma_start(
                out=out_1[groups, :, tokens, :].rearrange("g p m t -> p g (m t)").bitcast(I32), in_=codes[:].bitcast(I32)
            )
            if halves[-1] == 1:
                for q in range(4):
                    queue = nc.scalar if (tokens.stop == T and q % 2 == 0) else nc.sync
                    queue.dma_start(
                        out=out_2[:, 4 * q : 4 * q + 4, tokens].rearrange("g r m -> r g m").bitcast(I32),
                        in_=y_planes[first][32 * q : 32 * q + 4, :, :].bitcast(I32),
                    )

        both = [0, 1]

        widen(0, 5)
        turn_x(0)
        widen(1, 5)
        turn_x(1)
        nc.scalar.copy(
            out=bias[:].bitcast(F32).rearrange("p (n j) -> p n j", j=BIAS_WORDS), in_=spread[:].rearrange("p j n -> p n j")
        )
        widen(2, 8)
        turn_x(2)
        empty_x([0])
        widen(5, 8)
        quantize_x([0])
        empty_x([1])
        widen(6, 8)
        quantize_x([1])
        multiply(0, 1, 0)
        widen(3, 0)
        empty_x([2])
        turn_x(3)
        widen(7, 8)
        widen(8, 8)
        quantize_x([2])
        widen(4, 0)
        multiply(0, 0, 0)
        turn_x(4)
        turn_x(5)
        add_bias(0, 0)
        empty_x([3])
        tanh(0, 0)
        sigmoid(0, [0])
        empty_x([4, 5])
        widen(9, 8)
        quantize_x([3])
        widen(10, 8)
        multiply(0, 1, 1)
        multiply(0, 0, 1)
        widen(11, 8)

        last = TILES - 1
        low = slice(0, POOL_COLUMNS)
        high = slice(POOL_COLUMNS, N)
        turned = []
        for s in range(TILES):
            emptied = turned
            turned = [p for p in range(HEAD_TURNS, PAIRS) if (2 * p) // 3 == s + 3]
            if s >= 1:
                gate_mult("diff_low", s - 1, low)
                gate_mult("diff_high", s - 1, high)
                subtract(nc.gpsimd, "diff_low", 1, s, low)
                add_bias(s, 0)
            add_bias(s, 1)
            if s == 0:
                widen(12, 8)
                subtract(nc.vector, "diff_low", 1, s, low)
                quantize_x([4, 5])
            tanh(s, 1)
            if s < last:
                multiply(s + 1, 0, 0)
            for pair in turned:
                turn_x(pair)
            if s >= 2:
                turn_y(s - 2, both)
            if s < last:
                multiply(s + 1, 1, 0)
                multiply(s + 1, 1, 1)
                multiply(s + 1, 0, 1)
            if s == 0:
                sigmoid(s, [1])
            if s < last:
                tanh(s + 1, 0)
            if s == last:
                empty_y(s - 2, both)
            if s >= 1:
                sigmoid(s, both)
            if turned:
                empty_x(turned)
            if s == 0:
                widen(PAIRS - 2, 0)
                widen(PAIRS - 1, 0)
            if s >= 1:
                add_carry(s - 1, both)
            subtract(nc.vector, "diff_high", 2, s, high)
            if s >= 4 and s % 2 == 0:
                quantize_y(PLANE_BATCHES[(s - 4) // 2], both)
            if s >= 1:
                round_y(s - 1, both)
            if 2 <= s < last:
                empty_y(s - 2, both)
            if emptied:
                quantize_x(emptied)

        turn_y(last - 1, both)
        gate_mult("diff_low", last, low)
        gate_mult("diff_high", last, high)
        quantize_y(PLANE_BATCHES[-2], both)
        add_carry(last, [0])
        empty_y(last - 1, both)
        round_y(last, [0])
        turn_y(last, [0])
        closing = work.tile([P, HALF], BF16, name="closing", bufs=1)
        c = cols_of([1])
        nc.vector.tensor_tensor(out=closing[:], in0=f32_tile("step", last)[:, c], in1=carry_sb[last][:, c], op=ALU.add)
        bank = psum.tile([P, 2, P], F32, name="turn")
        for u in range(2):
            nc.tensor.transpose(bank[:, u, :], closing[:].bitcast(F32)[:, u::2], ident[:])
        y_bank[last, 1] = bank
        add_carry(last, [1])
        empty_y(last, [0])
        empty_y(last, [1])
        quantize_y(PLANE_BATCHES[-1], [0])
        quantize_y(PLANE_BATCHES[-1], [1])
